import numpy as np
import ml_dtypes


def mxq(x, axis, fmt="e4m3"):
    dtype, down = {"e4m3": (ml_dtypes.float8_e4m3fn, 7), "e5m2": (ml_dtypes.float8_e5m2, 14)}[fmt]
    v = np.moveaxis(np.asarray(x, np.float32).astype(ml_dtypes.bfloat16).astype(np.float64), axis, -1)
    blocks = v.reshape(v.shape[:-1] + (-1, 32))
    amax = np.abs(blocks).max(-1, keepdims=True)
    byte = np.maximum(np.where(amax > 0, np.frexp(amax)[1] - 1 + 127, 0) - down, 1)
    scale = np.exp2(byte - 127.0)
    codes = (blocks / scale).astype(np.float32).astype(dtype).astype(np.float64)
    return np.moveaxis((codes * scale).reshape(v.shape), -1, axis)


WIDE = False


def mx_kscale(k):
    if not WIDE:
        return np.ones(k)
    levels = np.array([10, -10, 5, -5, 0])
    if k % 512:
        return np.exp2(np.random.permutation(np.resize(levels, k // 32))).repeat(32)
    a = np.empty((k // 512, 16))
    for p in range(k // 512):
        a[p, :8] = np.random.permutation(np.resize(levels, 8))
        for g in range(8):
            far = levels[np.abs(levels - a[p, g]) >= 10]
            a[p, g + 8] = far[np.random.randint(len(far))]
    return np.exp2(a.ravel()).repeat(32)


def f64(x):
    return np.asarray(x).astype(np.float64)


def striped(idx):
    return np.tile(idx.reshape(-1, 16).T, (8, 1)).astype(np.uint16)


def unstriped(offs):
    return offs[:16].T.reshape(-1).astype(np.int64)


E2M1 = np.array([0.0, 0.5, 1.0, 1.5, 2.0, 3.0, 4.0, 6.0, -0.0, -0.5, -1.0, -1.5, -2.0, -3.0, -4.0, -6.0])


def pack_weight(w, fmt):
    k, n = w.shape
    w = f64(np.asarray(w, np.float32).astype(ml_dtypes.bfloat16)).reshape(k // 32, 32, n)
    amax = np.abs(w).max(1)
    if fmt == "e4m3":
        byte = np.frexp(amax)[1] - 1 + 127 - 7
    else:
        mant, ex = np.frexp(amax / 6.0)
        byte = np.where(mant > 0.5, ex, ex - 1) + 127
    byte = np.clip(np.where(amax > 0, byte, 1), 1, 254)
    scaled = (w * np.exp2(127.0 - byte)[:, None, :]).reshape(k, n).astype(np.float32)
    by_word = np.ascontiguousarray(scaled.reshape(k // 512, 128, 4, n).transpose(0, 1, 3, 2))
    if fmt == "e4m3":
        words = by_word.astype(ml_dtypes.float8_e4m3fn).view(np.uint8)
    else:
        c = by_word.astype(ml_dtypes.float4_e2m1fn).view(np.uint8) & 0xF
        words = (c[..., 0::2] | (c[..., 1::2] << 4)).reshape(k // 512, 128, 2 * n)
    return np.ascontiguousarray(words), np.ascontiguousarray(byte.astype(np.uint8).reshape(k // 512, 16, n))


def unpack_weight(words, scales, fmt):
    g, _, n = scales.shape
    words = np.ascontiguousarray(words).reshape(g, 128, n, -1)
    if fmt == "e4m3":
        vals = words.view(ml_dtypes.float8_e4m3fn).astype(np.float64)
    else:
        nib = np.empty((g, 128, n, 4), np.uint8)
        nib[..., 0::2] = words & 0xF
        nib[..., 1::2] = words >> 4
        vals = E2M1[nib]
    vals = vals * np.repeat(np.exp2(scales.astype(np.float64) - 127.0), 8, axis=1)[..., None]
    return vals.transpose(0, 1, 3, 2).reshape(g * 512, n)


def gelu(v):
    return 0.5 * v * (1.0 + np.tanh(np.sqrt(2.0 / np.pi) * (v + 0.044715 * v**3)))


K, T, S, H, S2, T3, T2 = 1024, 2048, 512, 1024, 512, 2048, 1024

def setup_inputs():
    n = np.random.standard_normal
    s = mx_kscale(K)[:, None]
    u = s
    tab_words, tab_scales = pack_weight(n((K, T)) * s, "e4m3")
    tab2_words, tab2_scales = pack_weight(n((H, T3)) / np.sqrt(H) / u, "e4m3")
    w4_words, w4_scales = pack_weight(0.56 * n((K, H)) / np.sqrt(K) / s, "e2m1")
    return {
        "tab_words": tab_words, "tab_scales": tab_scales,
        "offs": striped(np.random.permutation(T)[:S]),
        "tab2_words": tab2_words, "tab2_scales": tab2_scales,
        "offs2": striped(np.random.permutation(T3)[:S2]),
        "offs3": striped(np.random.permutation(T2)[:S]),
        "w4_words": w4_words, "w4_scales": w4_scales,
        "w1": (0.7 * n((K, H)) / np.sqrt(K) / s).astype(np.float32),
        "gain": (1.5 * np.exp(0.3 * n(H)) * u[:, 0]).astype(np.float32),
        "bias": (0.5 * n(S2)).astype(np.float32),
        "wgo": np.exp(0.3 * n((128, S))).astype(np.float32),
        "page1": (0.6 * n((S2, T2))).astype(np.float32),
    }

def reference(tab_words, tab_scales, offs, tab2_words, tab2_scales, offs2, offs3,
              w4_words, w4_scales, w1, gain, bias, wgo, page1):
    v = unpack_weight(tab_words, tab_scales, "e4m3")[:, unstriped(offs)]
    v2 = unpack_weight(tab2_words, tab2_scales, "e4m3")[:, unstriped(offs2)]
    w4 = unpack_weight(w4_words, w4_scales, "e2m1")
    bend = np.sin(w4.T @ v)
    line = mxq(f64(w1), 0, "e4m3").T @ v
    h = f64(gain)[:, None] * np.tanh(bend + line)
    e = v2.T @ mxq(h, 0, "e4m3")
    d = v2.T @ v
    grade = np.tanh(e + f64(bias)[:, None]) * d
    out = f64(page1).copy()
    out[:, unstriped(offs3)] = np.tile(f64(wgo), (S2 // 128, 1)) * grade
    return out

@@ -1,0 +1,270 @@
+import math
+from contextlib import ExitStack
+
+import concourse.mybir as mybir
+
+K, T, S, H, S2, T3, T2 = 1024, 2048, 512, 1024, 512, 2048, 1024
+FLOPS = 2 * (2 * K * H * S + 2 * H * S2 * S)
+
+F32 = mybir.dt.float32
+BF16 = mybir.dt.bfloat16
+I32 = mybir.dt.int32
+U32 = mybir.dt.uint32
+U16 = mybir.dt.uint16
+U8 = mybir.dt.uint8
+FP8X4 = mybir.dt.float8_e4m3fn_x4
+FP4X4 = mybir.dt.float4_e2m1fn_x4
+ACT = mybir.ActivationFunctionType
+ALU = mybir.AluOpType
+
+P = 128
+PACK = 4
+KP = P * PACK
+PASSES = K // KP
+JC = 128
+CHUNKS = S // JC
+MT = S2 // P
+VECTOR_CAST = {(0, 0): 0, (0, 1): 128, (1, 0): 64, (1, 1): 64}
+GROUPS = ((0, 2), (2, 3), (3, 4))
+
+
+def tile_list_pace_note_grading_kernel(
+    tc, tab_words, tab_scales, offs, tab2_words, tab2_scales, offs2, offs3,
+    w4_words, w4_scales, w1, gain, bias, wgo, page1, out,
+):
+    nc = tc.nc
+    with ExitStack() as ctx:
+        keep = ctx.enter_context(tc.tile_pool(name="keep", bufs=1))
+        ring = ctx.enter_context(tc.tile_pool(name="ring", bufs=4))
+        psum = ctx.enter_context(tc.psum_pool(name="psum", bufs=1))
+
+        def kept(shape, dtype, name):
+            return keep.tile(shape, dtype, name=name, align_bytes=64)
+
+        idx = kept([P, S // 16], U16, "idx")
+        idx2 = kept([P, S2 // 16], U16, "idx2")
+        idx3 = kept([P, S // 16], U16, "idx3")
+        tab_w = [kept([P, T], I32, "tab_w%d" % a) for a in range(PASSES)]
+        tab2_w = [kept([P, T3], I32, "tab2_w%d" % a) for a in range(PASSES)]
+        tab_s = kept([P, PASSES * T], U8, "tab_s")
+        tab2_s = kept([P, T3], U8, "tab2_s")
+        w4_w = kept([P, PASSES, 2 * H], U8, "w4_w")
+        w4_s = kept([P, PASSES, H], U8, "w4_s")
+        w4p_w = kept([P, PASSES * 2 * H], U8, "w4p_w")
+        w4p_s = kept([P, PASSES * H], U8, "w4p_s")
+        w1_raw = {(b, a): kept([P, PACK, KP], F32, "w1_raw%d%d" % (b, a)) for b in range(2) for a in range(PASSES)}
+        w1_bf = {(b, a): kept([P, PACK * KP], BF16, "w1_bf%d%d" % (b, a)) for b in range(2) for a in range(PASSES)}
+        w1_w = {(b, a): kept([P, KP], U32, "w1_w%d%d" % (b, a)) for b in range(2) for a in range(PASSES)}
+        w1_s = {(b, a): kept([P, KP], U8, "w1_s%d%d" % (b, a)) for b in range(2) for a in range(PASSES)}
+        v_w = [kept([P, S], U32, "v_w%d" % a) for a in range(PASSES)]
+        v2_w = [kept([P, S2], U32, "v2_w%d" % a) for a in range(PASSES)]
+        v_planes = [kept([P, S], U8, "v_s%d" % a) for a in range(PASSES)]
+        v2_s = kept([P, S2], U8, "v2_s")
+        h_w = [kept([P, S], U32, "h_w%d" % b) for b in range(2)]
+        h_s = [kept([P, S], U8, "h_s%d" % b) for b in range(2)]
+        gain_t = kept([P, 2, PACK], F32, "gain_t")
+        bias_t = kept([P, MT], F32, "bias_t")
+        wgo_t = kept([P, S], F32, "wgo_t")
+        dw = [kept([P, S], F32, "dw%d" % m) for m in range(MT)]
+        page = [kept([P, T2], F32, "page%d" % m) for m in range(MT)]
+        plus_one = kept([P, 1], F32, "plus_one")
+        minus_one = kept([P, 1], F32, "minus_one")
+        shift = kept([P, 1], F32, "shift")
+        wave = {(b, c): kept([P, PACK * JC], F32, "wave%d%d" % (b, c)) for b in range(2) for c in range(CHUNKS)}
+
+        def words(dram, a):
+            return dram[a].rearrange("p n t -> p (n t)").bitcast(I32)
+
+        def load_w1(b, a):
+            rows = w1[KP * a : KP * (a + 1), KP * b : KP * (b + 1)]
+            nc.sync.dma_start(out=w1_raw[b, a][:], in_=rows.rearrange("(p j) c -> p j c", j=PACK))
+
+        nc.vector.memset(tab_s[:].bitcast(I32), 0)
+        nc.gpsimd.memset(w4_s[:].rearrange("p a n -> p (a n)").bitcast(I32), 0)
+        nc.gpsimd.memset(tab2_s[:].bitcast(I32), 0)
+        nc.vector.memset(plus_one[:], 1.0)
+        nc.vector.memset(minus_one[:], -1.0)
+        nc.vector.tensor_scalar(out=shift[:], in0=plus_one[:], scalar1=-math.pi / 8, scalar2=None, op0=ALU.mult)
+        nc.sync.dma_start(idx[:], offs)
+        nc.sync.dma_start(out=w4_w[:].bitcast(I32), in_=w4_words.rearrange("a p n -> p a n").bitcast(I32))
+        for q in range(4):
+            nc.sync.dma_start(
+                out=tab_s[32 * q : 32 * q + 4, :].bitcast(I32).rearrange("r (a n) -> r a n", a=PASSES),
+                in_=tab_scales[:, 4 * q : 4 * q + 4, :].rearrange("a r n -> r a n").bitcast(I32),
+            )
+        for a in range(PASSES):
+            nc.sync.dma_start(out=tab_w[a][:], in_=words(tab_words, a))
+        for q in range(4):
+            nc.sync.dma_start(
+                out=w4_s[32 * q : 32 * q + 4].bitcast(I32),
+                in_=w4_scales[:, 4 * q : 4 * q + 4, :].rearrange("a r n -> r a n").bitcast(I32),
+            )
+        load_w1(0, 0)
+        load_w1(0, 1)
+        nc.sync.dma_start(idx2[:], offs2)
+        for q in range(4):
+            nc.sync.dma_start(
+                out=tab2_s[32 * q : 32 * q + 8, :].bitcast(I32),
+                in_=tab2_scales[:, 4 * q : 4 * q + 4, :].bitcast(I32),
+            )
+        with nc.allow_non_contiguous_dma(reason="one short row of channels a partition"):
+            nc.sync.dma_start(out=gain_t[:], in_=gain.rearrange("(b p i) -> p b i", b=2, i=PACK))
+        nc.sync.dma_start(out=tab2_w[0][:], in_=words(tab2_words, 0))
+        load_w1(1, 0)
+        nc.sync.dma_start(out=tab2_w[1][:], in_=words(tab2_words, 1))
+        nc.sync.dma_start(out=wgo_t[:], in_=wgo)
+        load_w1(1, 1)
+        nc.sync.dma_start(idx3[:], offs3)
+        with nc.allow_non_contiguous_dma(reason="one value a partition and tile of templates"):
+            nc.sync.dma_start(out=bias_t[:], in_=bias.rearrange("(m p) -> p m", p=P))
+        for m in range(MT):
+            nc.sync.dma_start(out=page[m][:], in_=page1[P * m : P * (m + 1), :])
+
+        nc.vector.tensor_copy(
+            out=w4p_w[:].bitcast(U16).rearrange("p (g t m) -> p g t m", t=PACK, m=P),
+            in_=w4_w[:].rearrange("p a n -> p (a n)").bitcast(U16).rearrange("p (g m t) -> p g t m", t=PACK, m=P),
+        )
+        for a in range(PASSES):
+            nc.vector.tensor_copy(v_planes[a][:], tab_s[:, T * a : T * (a + 1)].indirect(idx[:]))
+        nc.vector.tensor_copy(v_w[0][:], tab_w[0][:].bitcast(U32).indirect(idx[:]))
+        nc.vector.tensor_copy(
+            out=w4p_s[:].rearrange("p (g t m) -> p g t m", t=PACK, m=P),
+            in_=w4_s[:].rearrange("p a n -> p (a n)").rearrange("p (g m t) -> p g t m", t=PACK, m=P),
+        )
+        nc.vector.tensor_copy(v_w[1][:], tab_w[1][:].bitcast(U32).indirect(idx[:]))
+
+        def cast_w1(b, a):
+            src = w1_raw[b, a][:].rearrange("p j (m t) -> p m j t", t=PACK)
+            dst = w1_bf[b, a][:].rearrange("p (t m j) -> p m j t", t=PACK, j=PACK)
+            cut = VECTOR_CAST[b, a]
+            if cut > 0:
+                nc.vector.tensor_copy(out=dst[:, 0:cut], in_=src[:, 0:cut])
+            if cut < P:
+                nc.scalar.copy(out=dst[:, cut:P], in_=src[:, cut:P])
+
+        def quantize_w1(b, a):
+            nc.vector.quantize_mx(out=w1_w[b, a][:].bitcast(FP8X4), scales=w1_s[b, a][:], in_=w1_bf[b, a][:])
+
+        def bend(b, c):
+            cols = slice(JC * c, JC * (c + 1))
+            bank = psum.tile([P, PACK, JC], F32, name="bend_bank", tag="bend", bufs=3)
+            for t in range(PACK):
+                for a in range(PASSES):
+                    col = H * a + KP * b + P * t
+                    nc.tensor.matmul_mx(
+                        out=bank[:, t, :],
+                        lhsT=w4p_w[:, 2 * col : 2 * (col + P)].bitcast(FP4X4),
+                        lhsT_scale=w4p_s[:, col : col + P],
+                        rhs=v_w[a][:, cols].bitcast(FP8X4),
+                        rhs_scale=v_planes[a][:, cols],
+                        start=(a == 0),
+                        stop=(a == PASSES - 1),
+                    )
+            x = wave[b, c]
+            nc.scalar.activation(
+                out=x[:].rearrange("p (n t) -> p n t", t=PACK),
+                in_=bank[:].rearrange("p t n -> p n t"),
+                func=ACT.Sin, scale=0.25, bias=shift[:],
+            )
+            nc.scalar.activation(out=x[:], in_=x[:], func=ACT.Square)
+            nc.scalar.activation(out=x[:], in_=x[:], func=ACT.Square, scale=-2.0, bias=plus_one[:])
+
+        def features(b, c):
+            cols = slice(JC * c, JC * (c + 1))
+            bank = psum.tile([P, PACK, JC], F32, name="line_bank", tag="line", bufs=3)
+            for t in range(PACK):
+                for a in range(PASSES):
+                    nc.tensor.matmul_mx(
+                        out=bank[:, t, :],
+                        lhsT=w1_w[b, a][:, P * t : P * (t + 1)].bitcast(FP8X4),
+                        lhsT_scale=w1_s[b, a][:, P * t : P * (t + 1)],
+                        rhs=v_w[a][:, cols].bitcast(FP8X4),
+                        rhs_scale=v_planes[a][:, cols],
+                        start=(a == 0),
+                        stop=(a == PASSES - 1),
+                    )
+            u = ring.tile([P, JC, PACK], F32, name="u", align_bytes=64)
+            nc.vector.scalar_tensor_tensor(
+                out=u[:],
+                in0=wave[b, c][:].rearrange("p (n t) -> p n t", t=PACK),
+                scalar=2.0,
+                in1=bank[:].rearrange("p t n -> p n t"),
+                op0=ALU.mult,
+                op1=ALU.add,
+            )
+            nc.scalar.activation(out=u[:], in_=u[:], func=ACT.Tanh, bias=minus_one[:])
+            h_bf = ring.tile([P, JC, PACK], BF16, name="h_bf", align_bytes=64)
+            nc.vector.tensor_tensor(
+                out=h_bf[:],
+                in0=u[:],
+                in1=gain_t[:, b, :].unsqueeze(1).to_broadcast([P, JC, PACK]),
+                op=ALU.mult,
+            )
+            nc.vector.quantize_mx(
+                out=h_w[b][:, cols].bitcast(FP8X4),
+                scales=h_s[b][:, cols],
+                in_=h_bf[:].rearrange("p n t -> p (n t)"),
+            )
+
+        def direct(m):
+            rows = slice(P * m, P * (m + 1))
+            bank = psum.tile([P, S], F32, name="d_bank", tag="score", bufs=2)
+            for a in range(PASSES):
+                nc.tensor.matmul_mx(
+                    out=bank[:],
+                    lhsT=v2_w[a][:, rows].bitcast(FP8X4),
+                    lhsT_scale=v2_s[4 * a : P, rows],
+                    rhs=v_w[a][:].bitcast(FP8X4),
+                    rhs_scale=v_planes[a][:],
+                    start=(a == 0),
+                    stop=(a == PASSES - 1),
+                )
+            nc.vector.tensor_tensor(out=dw[m][:], in0=bank[:], in1=wgo_t[:], op=ALU.mult)
+
+        def grade(m, c0, c1):
+            rows = slice(P * m, P * (m + 1))
+            cols = slice(JC * c0, JC * c1)
+            width = JC * (c1 - c0)
+            bank = psum.tile([P, S], F32, name="e_bank", tag="score", bufs=2)
+            for b in range(2):
+                nc.tensor.matmul_mx(
+                    out=bank[:, 0:width],
+                    lhsT=v2_w[b][:, rows].bitcast(FP8X4),
+                    lhsT_scale=v2_s[4 * b : P, rows],
+                    rhs=h_w[b][:, cols].bitcast(FP8X4),
+                    rhs_scale=h_s[b][:, cols],
+                    start=(b == 0),
+                    stop=(b == 1),
+                )
+            score = ring.tile([P, 2 * JC], F32, name="score", align_bytes=64)
+            nc.scalar.activation(out=score[:, 0:width], in_=bank[:, 0:width], func=ACT.Tanh, bias=bias_t[:, m : m + 1])
+            nc.vector.tensor_tensor(
+                page[m][:].indirect(idx3[:, JC * c0 // 16 : JC * c1 // 16]),
+                score[:, 0:width],
+                dw[m][:, cols],
+                ALU.mult,
+            )
+
+        for b in range(2):
+            for a in range(PASSES):
+                cast_w1(b, a)
+                quantize_w1(b, a)
+        for c in range(CHUNKS):
+            bend(0, c)
+        for c in range(CHUNKS):
+            features(0, c)
+        nc.vector.tensor_copy(v2_s[:], tab2_s[:].indirect(idx2[:]))
+        for a in range(PASSES):
+            nc.vector.tensor_copy(v2_w[a][:], tab2_w[a][:].bitcast(U32).indirect(idx2[:]))
+        for m in range(MT):
+            direct(m)
+        done = 0
+        for c0, c1 in GROUPS:
+            for c in range(done, min(c1 + 1, CHUNKS)):
+                bend(1, c)
+                features(1, c)
+                done = c + 1
+            for m in range(MT):
+                grade(m, c0, c1)
+                if c1 == CHUNKS:
+                    nc.sync.dma_start(out=out[P * m : P * (m + 1), :], in_=page[m][:])

@@ -85,6 +85,8 @@ def tile_list_pace_note_grading_kernel(
         nc.vector.memset(plus_one[:], 1.0)
         nc.vector.memset(minus_one[:], -1.0)
         nc.vector.tensor_scalar(out=shift[:], in0=plus_one[:], scalar1=-math.pi / 8, scalar2=None, op0=ALU.mult)
+        warm = kept([P, 1], F32, "warm")
+        nc.scalar.activation(out=warm[:], in_=plus_one[:], func=ACT.Silu)
         nc.sync.dma_start(idx[:], offs)
         nc.sync.dma_start(out=w4_w[:].bitcast(I32), in_=w4_words.rearrange("a p n -> p a n").bitcast(I32))
         for q in range(4):

@@ -24,8 +24,9 @@ PASSES = K // KP
 JC = 128
 CHUNKS = S // JC
 MT = S2 // P
-VECTOR_CAST = {(0, 0): 0, (0, 1): 128, (1, 0): 64, (1, 1): 64}
-GROUPS = ((0, 2), (2, 3), (3, 4))
+NWAVE = 2
+VECTOR_CAST = {(0, 0): 128, (0, 1): 128, (1, 0): 32, (1, 1): 96}
+GROUPS = ((0, 2), (2, 4))
 
 
 def tile_list_pace_note_grading_kernel(
@@ -35,7 +36,6 @@ def tile_list_pace_note_grading_kernel(
     nc = tc.nc
     with ExitStack() as ctx:
         keep = ctx.enter_context(tc.tile_pool(name="keep", bufs=1))
-        ring = ctx.enter_context(tc.tile_pool(name="ring", bufs=4))
         psum = ctx.enter_context(tc.psum_pool(name="psum", bufs=1))
 
         def kept(shape, dtype, name):
@@ -70,7 +70,12 @@ def tile_list_pace_note_grading_kernel(
         plus_one = kept([P, 1], F32, "plus_one")
         minus_one = kept([P, 1], F32, "minus_one")
         shift = kept([P, 1], F32, "shift")
-        wave = {(b, c): kept([P, PACK * JC], F32, "wave%d%d" % (b, c)) for b in range(2) for c in range(CHUNKS)}
+        wave = [kept([P, PACK * JC], F32, "wave%d" % i) for i in range(NWAVE)]
+        u_tiles = [kept([P, PACK * JC], F32, "u%d" % i) for i in range(4)]
+        h_tiles = [kept([P, PACK * JC], BF16, "h_bf%d" % i) for i in range(3)]
+        bend_banks = [psum.tile([P, PACK, JC], F32, name="bend_bank%d" % i) for i in range(3)]
+        line_banks = [psum.tile([P, PACK, JC], F32, name="line_bank%d" % i) for i in range(3)]
+        score_banks = [psum.tile([P, S], F32, name="score_bank%d" % i) for i in range(2)]
 
         def words(dram, a):
             return dram[a].rearrange("p n t -> p (n t)").bitcast(I32)
@@ -103,19 +108,19 @@ def tile_list_pace_note_grading_kernel(
             )
         load_w1(0, 0)
         load_w1(0, 1)
+        with nc.allow_non_contiguous_dma(reason="one short row of channels a partition"):
+            nc.sync.dma_start(out=gain_t[:], in_=gain.rearrange("(b p i) -> p b i", b=2, i=PACK))
+        load_w1(1, 0)
         nc.sync.dma_start(idx2[:], offs2)
         for q in range(4):
             nc.sync.dma_start(
                 out=tab2_s[32 * q : 32 * q + 8, :].bitcast(I32),
                 in_=tab2_scales[:, 4 * q : 4 * q + 4, :].bitcast(I32),
             )
-        with nc.allow_non_contiguous_dma(reason="one short row of channels a partition"):
-            nc.sync.dma_start(out=gain_t[:], in_=gain.rearrange("(b p i) -> p b i", b=2, i=PACK))
         nc.sync.dma_start(out=tab2_w[0][:], in_=words(tab2_words, 0))
-        load_w1(1, 0)
+        load_w1(1, 1)
         nc.sync.dma_start(out=tab2_w[1][:], in_=words(tab2_words, 1))
         nc.sync.dma_start(out=wgo_t[:], in_=wgo)
-        load_w1(1, 1)
         nc.sync.dma_start(idx3[:], offs3)
         with nc.allow_non_contiguous_dma(reason="one value a partition and tile of templates"):
             nc.sync.dma_start(out=bias_t[:], in_=bias.rearrange("(m p) -> p m", p=P))
@@ -149,7 +154,8 @@ def tile_list_pace_note_grading_kernel(
 
         def bend(b, c):
             cols = slice(JC * c, JC * (c + 1))
-            bank = psum.tile([P, PACK, JC], F32, name="bend_bank", tag="bend", bufs=3)
+            unit = CHUNKS * b + c
+            bank = bend_banks[unit % 3]
             for t in range(PACK):
                 for a in range(PASSES):
                     col = H * a + KP * b + P * t
@@ -162,7 +168,7 @@ def tile_list_pace_note_grading_kernel(
                         start=(a == 0),
                         stop=(a == PASSES - 1),
                     )
-            x = wave[b, c]
+            x = wave[unit % NWAVE]
             nc.scalar.activation(
                 out=x[:].rearrange("p (n t) -> p n t", t=PACK),
                 in_=bank[:].rearrange("p t n -> p n t"),
@@ -173,7 +179,8 @@ def tile_list_pace_note_grading_kernel(
 
         def features(b, c):
             cols = slice(JC * c, JC * (c + 1))
-            bank = psum.tile([P, PACK, JC], F32, name="line_bank", tag="line", bufs=3)
+            unit = CHUNKS * b + c
+            bank = line_banks[unit % 3]
             for t in range(PACK):
                 for a in range(PASSES):
                     nc.tensor.matmul_mx(
@@ -185,32 +192,32 @@ def tile_list_pace_note_grading_kernel(
                         start=(a == 0),
                         stop=(a == PASSES - 1),
                     )
-            u = ring.tile([P, JC, PACK], F32, name="u", align_bytes=64)
+            u = u_tiles[unit % 4][:].rearrange("p (n t) -> p n t", t=PACK)
             nc.vector.scalar_tensor_tensor(
-                out=u[:],
-                in0=wave[b, c][:].rearrange("p (n t) -> p n t", t=PACK),
+                out=u,
+                in0=wave[unit % NWAVE][:].rearrange("p (n t) -> p n t", t=PACK),
                 scalar=2.0,
                 in1=bank[:].rearrange("p t n -> p n t"),
                 op0=ALU.mult,
                 op1=ALU.add,
             )
-            nc.scalar.activation(out=u[:], in_=u[:], func=ACT.Tanh, bias=minus_one[:])
-            h_bf = ring.tile([P, JC, PACK], BF16, name="h_bf", align_bytes=64)
+            nc.scalar.activation(out=u, in_=u, func=ACT.Tanh, bias=minus_one[:])
+            h_bf = h_tiles[unit % 3]
             nc.vector.tensor_tensor(
-                out=h_bf[:],
-                in0=u[:],
+                out=h_bf[:].rearrange("p (n t) -> p n t", t=PACK),
+                in0=u,
                 in1=gain_t[:, b, :].unsqueeze(1).to_broadcast([P, JC, PACK]),
                 op=ALU.mult,
             )
             nc.vector.quantize_mx(
                 out=h_w[b][:, cols].bitcast(FP8X4),
                 scales=h_s[b][:, cols],
-                in_=h_bf[:].rearrange("p n t -> p (n t)"),
+                in_=h_bf[:],
             )
 
         def direct(m):
             rows = slice(P * m, P * (m + 1))
-            bank = psum.tile([P, S], F32, name="d_bank", tag="score", bufs=2)
+            bank = score_banks[m % 2]
             for a in range(PASSES):
                 nc.tensor.matmul_mx(
                     out=bank[:],
@@ -227,7 +234,7 @@ def tile_list_pace_note_grading_kernel(
             rows = slice(P * m, P * (m + 1))
             cols = slice(JC * c0, JC * c1)
             width = JC * (c1 - c0)
-            bank = psum.tile([P, S], F32, name="e_bank", tag="score", bufs=2)
+            bank = score_banks[m % 2]
             for b in range(2):
                 nc.tensor.matmul_mx(
                     out=bank[:, 0:width],
@@ -238,34 +245,32 @@ def tile_list_pace_note_grading_kernel(
                     start=(b == 0),
                     stop=(b == 1),
                 )
-            score = ring.tile([P, 2 * JC], F32, name="score", align_bytes=64)
-            nc.scalar.activation(out=score[:, 0:width], in_=bank[:, 0:width], func=ACT.Tanh, bias=bias_t[:, m : m + 1])
+            tile_of = {(0, 0): 1, (0, 1): 3, (2, 0): 0, (2, 1): 2}[c0, m // 2]
+            score = u_tiles[tile_of][:, width * (m % 2) : width * (m % 2 + 1)]
+            nc.scalar.activation(out=score, in_=bank[:, 0:width], func=ACT.Tanh, bias=bias_t[:, m : m + 1])
             nc.vector.tensor_tensor(
                 page[m][:].indirect(idx3[:, JC * c0 // 16 : JC * c1 // 16]),
-                score[:, 0:width],
+                score,
                 dw[m][:, cols],
                 ALU.mult,
             )
 
-        for b in range(2):
-            for a in range(PASSES):
-                cast_w1(b, a)
-                quantize_w1(b, a)
-        for c in range(CHUNKS):
-            bend(0, c)
-        for c in range(CHUNKS):
-            features(0, c)
         nc.vector.tensor_copy(v2_s[:], tab2_s[:].indirect(idx2[:]))
         for a in range(PASSES):
             nc.vector.tensor_copy(v2_w[a][:], tab2_w[a][:].bitcast(U32).indirect(idx2[:]))
         for m in range(MT):
             direct(m)
-        done = 0
+        for b in range(2):
+            for a in range(PASSES):
+                cast_w1(b, a)
+                quantize_w1(b, a)
+        units = [(b, c) for b in range(2) for c in range(CHUNKS)]
+        bend(*units[0])
+        for i, unit in enumerate(units):
+            if i + 1 < len(units):
+                bend(*units[i + 1])
+            features(*unit)
         for c0, c1 in GROUPS:
-            for c in range(done, min(c1 + 1, CHUNKS)):
-                bend(1, c)
-                features(1, c)
-                done = c + 1
             for m in range(MT):
                 grade(m, c0, c1)
                 if c1 == CHUNKS:

@@ -21,12 +21,21 @@ P = 128
 PACK = 4
 KP = P * PACK
 PASSES = K // KP
+HALVES = H // KP
+QUADS = 4
+LIST_ROWS = 16
 JC = 128
 CHUNKS = S // JC
+UNITS = HALVES * CHUNKS
 MT = S2 // P
-NWAVE = 2
-VECTOR_CAST = {(0, 0): 128, (0, 1): 128, (1, 0): 32, (1, 1): 96}
-GROUPS = ((0, 2), (2, 4))
+GROUP = 2 * JC
+
+VECTOR_CAST = {(0, 0): 128, (0, 1): 128, (1, 0): 0, (1, 1): 96}
+
+SINE_TILES = 2
+SUM_TILES = 4
+H_TILES = 3
+BEND_BANKS, LINE_BANKS, SCORE_BANKS = 3, 3, 2
 
 
 def tile_list_pace_note_grading_kernel(
@@ -41,44 +50,46 @@ def tile_list_pace_note_grading_kernel(
         def kept(shape, dtype, name):
             return keep.tile(shape, dtype, name=name, align_bytes=64)
 
-        idx = kept([P, S // 16], U16, "idx")
-        idx2 = kept([P, S2 // 16], U16, "idx2")
-        idx3 = kept([P, S // 16], U16, "idx3")
+        blocks = [(b, a) for b in range(HALVES) for a in range(PASSES)]
+        idx = kept([P, S // LIST_ROWS], U16, "idx")
+        idx2 = kept([P, S2 // LIST_ROWS], U16, "idx2")
+        idx3 = kept([P, S // LIST_ROWS], U16, "idx3")
         tab_w = [kept([P, T], I32, "tab_w%d" % a) for a in range(PASSES)]
-        tab2_w = [kept([P, T3], I32, "tab2_w%d" % a) for a in range(PASSES)]
+        tab2_w = [kept([P, T3], I32, "tab2_w%d" % b) for b in range(HALVES)]
         tab_s = kept([P, PASSES * T], U8, "tab_s")
         tab2_s = kept([P, T3], U8, "tab2_s")
         w4_w = kept([P, PASSES, 2 * H], U8, "w4_w")
         w4_s = kept([P, PASSES, H], U8, "w4_s")
-        w4p_w = kept([P, PASSES * 2 * H], U8, "w4p_w")
-        w4p_s = kept([P, PASSES * H], U8, "w4p_s")
-        w1_raw = {(b, a): kept([P, PACK, KP], F32, "w1_raw%d%d" % (b, a)) for b in range(2) for a in range(PASSES)}
-        w1_bf = {(b, a): kept([P, PACK * KP], BF16, "w1_bf%d%d" % (b, a)) for b in range(2) for a in range(PASSES)}
-        w1_w = {(b, a): kept([P, KP], U32, "w1_w%d%d" % (b, a)) for b in range(2) for a in range(PASSES)}
-        w1_s = {(b, a): kept([P, KP], U8, "w1_s%d%d" % (b, a)) for b in range(2) for a in range(PASSES)}
+        w4_dealt_w = kept([P, PASSES * 2 * H], U8, "w4_dealt_w")
+        w4_dealt_s = kept([P, PASSES * H], U8, "w4_dealt_s")
+        w1_raw = {ba: kept([P, PACK, KP], F32, "w1_raw%d%d" % ba) for ba in blocks}
+        w1_bf = {ba: kept([P, PACK * KP], BF16, "w1_bf%d%d" % ba) for ba in blocks}
+        w1_w = {ba: kept([P, KP], U32, "w1_w%d%d" % ba) for ba in blocks}
+        w1_s = {ba: kept([P, KP], U8, "w1_s%d%d" % ba) for ba in blocks}
         v_w = [kept([P, S], U32, "v_w%d" % a) for a in range(PASSES)]
-        v2_w = [kept([P, S2], U32, "v2_w%d" % a) for a in range(PASSES)]
-        v_planes = [kept([P, S], U8, "v_s%d" % a) for a in range(PASSES)]
+        v2_w = [kept([P, S2], U32, "v2_w%d" % b) for b in range(HALVES)]
+        v_s = [kept([P, S], U8, "v_s%d" % a) for a in range(PASSES)]
         v2_s = kept([P, S2], U8, "v2_s")
-        h_w = [kept([P, S], U32, "h_w%d" % b) for b in range(2)]
-        h_s = [kept([P, S], U8, "h_s%d" % b) for b in range(2)]
-        gain_t = kept([P, 2, PACK], F32, "gain_t")
+        h_w = [kept([P, S], U32, "h_w%d" % b) for b in range(HALVES)]
+        h_s = [kept([P, S], U8, "h_s%d" % b) for b in range(HALVES)]
+        gain_t = kept([P, HALVES, PACK], F32, "gain_t")
         bias_t = kept([P, MT], F32, "bias_t")
         wgo_t = kept([P, S], F32, "wgo_t")
-        dw = [kept([P, S], F32, "dw%d" % m) for m in range(MT)]
+        d_wgo = [kept([P, S], F32, "d_wgo%d" % m) for m in range(MT)]
         page = [kept([P, T2], F32, "page%d" % m) for m in range(MT)]
         plus_one = kept([P, 1], F32, "plus_one")
         minus_one = kept([P, 1], F32, "minus_one")
         shift = kept([P, 1], F32, "shift")
-        wave = [kept([P, PACK * JC], F32, "wave%d" % i) for i in range(NWAVE)]
-        u_tiles = [kept([P, PACK * JC], F32, "u%d" % i) for i in range(4)]
-        h_tiles = [kept([P, PACK * JC], BF16, "h_bf%d" % i) for i in range(3)]
-        bend_banks = [psum.tile([P, PACK, JC], F32, name="bend_bank%d" % i) for i in range(3)]
-        line_banks = [psum.tile([P, PACK, JC], F32, name="line_bank%d" % i) for i in range(3)]
-        score_banks = [psum.tile([P, S], F32, name="score_bank%d" % i) for i in range(2)]
+        sine_tiles = [kept([P, PACK * JC], F32, "sine%d" % n) for n in range(SINE_TILES)]
+        sum_tiles = [kept([P, PACK * JC], F32, "sum%d" % n) for n in range(SUM_TILES)]
+        h_tiles = [kept([P, PACK * JC], BF16, "h_bf%d" % n) for n in range(H_TILES)]
+        h_by_deal = kept([P, PACK, JC], BF16, "h_by_deal")
+        bend_banks = [psum.tile([P, PACK, JC], F32, name="bend_bank%d" % n) for n in range(BEND_BANKS)]
+        line_banks = [psum.tile([P, PACK, JC], F32, name="line_bank%d" % n) for n in range(LINE_BANKS)]
+        score_banks = [psum.tile([P, S], F32, name="score_bank%d" % n) for n in range(SCORE_BANKS)]
 
         def words(dram, a):
-            return dram[a].rearrange("p n t -> p (n t)").bitcast(I32)
+            return dram[a].rearrange("p n i -> p (n i)").bitcast(I32)
 
         def load_w1(b, a):
             rows = w1[KP * a : KP * (a + 1), KP * b : KP * (b + 1)]
@@ -92,27 +103,28 @@ def tile_list_pace_note_grading_kernel(
         nc.vector.tensor_scalar(out=shift[:], in0=plus_one[:], scalar1=-math.pi / 8, scalar2=None, op0=ALU.mult)
         warm = kept([P, 1], F32, "warm")
         nc.scalar.activation(out=warm[:], in_=plus_one[:], func=ACT.Silu)
+
         nc.sync.dma_start(idx[:], offs)
         nc.sync.dma_start(out=w4_w[:].bitcast(I32), in_=w4_words.rearrange("a p n -> p a n").bitcast(I32))
-        for q in range(4):
+        for q in range(QUADS):
             nc.sync.dma_start(
                 out=tab_s[32 * q : 32 * q + 4, :].bitcast(I32).rearrange("r (a n) -> r a n", a=PASSES),
                 in_=tab_scales[:, 4 * q : 4 * q + 4, :].rearrange("a r n -> r a n").bitcast(I32),
             )
         for a in range(PASSES):
             nc.sync.dma_start(out=tab_w[a][:], in_=words(tab_words, a))
-        for q in range(4):
+        for q in range(QUADS):
             nc.sync.dma_start(
                 out=w4_s[32 * q : 32 * q + 4].bitcast(I32),
                 in_=w4_scales[:, 4 * q : 4 * q + 4, :].rearrange("a r n -> r a n").bitcast(I32),
             )
         load_w1(0, 0)
         load_w1(0, 1)
-        with nc.allow_non_contiguous_dma(reason="one short row of channels a partition"):
-            nc.sync.dma_start(out=gain_t[:], in_=gain.rearrange("(b p i) -> p b i", b=2, i=PACK))
+        with nc.allow_non_contiguous_dma(reason="the four channels of a partition's word, for each half"):
+            nc.sync.dma_start(out=gain_t[:], in_=gain.rearrange("(b p i) -> p b i", b=HALVES, i=PACK))
         load_w1(1, 0)
         nc.sync.dma_start(idx2[:], offs2)
-        for q in range(4):
+        for q in range(QUADS):
             nc.sync.dma_start(
                 out=tab2_s[32 * q : 32 * q + 8, :].bitcast(I32),
                 in_=tab2_scales[:, 4 * q : 4 * q + 4, :].bitcast(I32),
@@ -122,93 +134,100 @@ def tile_list_pace_note_grading_kernel(
         nc.sync.dma_start(out=tab2_w[1][:], in_=words(tab2_words, 1))
         nc.sync.dma_start(out=wgo_t[:], in_=wgo)
         nc.sync.dma_start(idx3[:], offs3)
-        with nc.allow_non_contiguous_dma(reason="one value a partition and tile of templates"):
+        with nc.allow_non_contiguous_dma(reason="one value a partition for each tile of templates"):
             nc.sync.dma_start(out=bias_t[:], in_=bias.rearrange("(m p) -> p m", p=P))
         for m in range(MT):
             nc.sync.dma_start(out=page[m][:], in_=page1[P * m : P * (m + 1), :])
 
         nc.vector.tensor_copy(
-            out=w4p_w[:].bitcast(U16).rearrange("p (g t m) -> p g t m", t=PACK, m=P),
-            in_=w4_w[:].rearrange("p a n -> p (a n)").bitcast(U16).rearrange("p (g m t) -> p g t m", t=PACK, m=P),
+            out=w4_dealt_w[:].bitcast(U16).rearrange("p (g i c) -> p g i c", i=PACK, c=P),
+            in_=w4_w[:].rearrange("p a n -> p (a n)").bitcast(U16).rearrange("p (g c i) -> p g i c", i=PACK, c=P),
         )
         for a in range(PASSES):
-            nc.vector.tensor_copy(v_planes[a][:], tab_s[:, T * a : T * (a + 1)].indirect(idx[:]))
+            nc.vector.tensor_copy(v_s[a][:], tab_s[:, T * a : T * (a + 1)].indirect(idx[:]))
         nc.vector.tensor_copy(v_w[0][:], tab_w[0][:].bitcast(U32).indirect(idx[:]))
         nc.vector.tensor_copy(
-            out=w4p_s[:].rearrange("p (g t m) -> p g t m", t=PACK, m=P),
-            in_=w4_s[:].rearrange("p a n -> p (a n)").rearrange("p (g m t) -> p g t m", t=PACK, m=P),
+            out=w4_dealt_s[:].rearrange("p (g i c) -> p g i c", i=PACK, c=P),
+            in_=w4_s[:].rearrange("p a n -> p (a n)").rearrange("p (g c i) -> p g i c", i=PACK, c=P),
         )
         nc.vector.tensor_copy(v_w[1][:], tab_w[1][:].bitcast(U32).indirect(idx[:]))
 
-        def cast_w1(b, a):
-            src = w1_raw[b, a][:].rearrange("p j (m t) -> p m j t", t=PACK)
-            dst = w1_bf[b, a][:].rearrange("p (t m j) -> p m j t", t=PACK, j=PACK)
+        def quantize_w1(b, a):
+            src = w1_raw[b, a][:].rearrange("p j (c i) -> p c j i", i=PACK)
+            dst = w1_bf[b, a][:].rearrange("p (i c j) -> p c j i", i=PACK, j=PACK)
             cut = VECTOR_CAST[b, a]
             if cut > 0:
                 nc.vector.tensor_copy(out=dst[:, 0:cut], in_=src[:, 0:cut])
             if cut < P:
                 nc.scalar.copy(out=dst[:, cut:P], in_=src[:, cut:P])
-
-        def quantize_w1(b, a):
             nc.vector.quantize_mx(out=w1_w[b, a][:].bitcast(FP8X4), scales=w1_s[b, a][:], in_=w1_bf[b, a][:])
 
-        def bend(b, c):
-            cols = slice(JC * c, JC * (c + 1))
-            unit = CHUNKS * b + c
-            bank = bend_banks[unit % 3]
-            for t in range(PACK):
+        def bend(unit):
+            b, chunk = divmod(unit, CHUNKS)
+            cols = slice(JC * chunk, JC * (chunk + 1))
+            bank = bend_banks[unit % BEND_BANKS]
+            for i in range(PACK):
                 for a in range(PASSES):
-                    col = H * a + KP * b + P * t
+                    col = H * a + KP * b + P * i
                     nc.tensor.matmul_mx(
-                        out=bank[:, t, :],
-                        lhsT=w4p_w[:, 2 * col : 2 * (col + P)].bitcast(FP4X4),
-                        lhsT_scale=w4p_s[:, col : col + P],
+                        out=bank[:, i, :],
+                        lhsT=w4_dealt_w[:, 2 * col : 2 * (col + P)].bitcast(FP4X4),
+                        lhsT_scale=w4_dealt_s[:, col : col + P],
                         rhs=v_w[a][:, cols].bitcast(FP8X4),
-                        rhs_scale=v_planes[a][:, cols],
+                        rhs_scale=v_s[a][:, cols],
                         start=(a == 0),
                         stop=(a == PASSES - 1),
                     )
-            x = wave[unit % NWAVE]
+            sine = sine_tiles[unit % SINE_TILES]
             nc.scalar.activation(
-                out=x[:].rearrange("p (n t) -> p n t", t=PACK),
-                in_=bank[:].rearrange("p t n -> p n t"),
+                out=sine[:].rearrange("p (n i) -> p n i", i=PACK),
+                in_=bank[:].rearrange("p i n -> p n i"),
                 func=ACT.Sin, scale=0.25, bias=shift[:],
             )
-            nc.scalar.activation(out=x[:], in_=x[:], func=ACT.Square)
-            nc.scalar.activation(out=x[:], in_=x[:], func=ACT.Square, scale=-2.0, bias=plus_one[:])
+            nc.scalar.activation(out=sine[:], in_=sine[:], func=ACT.Square)
+            nc.scalar.activation(out=sine[:], in_=sine[:], func=ACT.Square, scale=-2.0, bias=plus_one[:])
 
-        def features(b, c):
-            cols = slice(JC * c, JC * (c + 1))
-            unit = CHUNKS * b + c
-            bank = line_banks[unit % 3]
-            for t in range(PACK):
+        def features(unit):
+            b, chunk = divmod(unit, CHUNKS)
+            cols = slice(JC * chunk, JC * (chunk + 1))
+            bank = line_banks[unit % LINE_BANKS]
+            for i in range(PACK):
                 for a in range(PASSES):
                     nc.tensor.matmul_mx(
-                        out=bank[:, t, :],
-                        lhsT=w1_w[b, a][:, P * t : P * (t + 1)].bitcast(FP8X4),
-                        lhsT_scale=w1_s[b, a][:, P * t : P * (t + 1)],
+                        out=bank[:, i, :],
+                        lhsT=w1_w[b, a][:, P * i : P * (i + 1)].bitcast(FP8X4),
+                        lhsT_scale=w1_s[b, a][:, P * i : P * (i + 1)],
                         rhs=v_w[a][:, cols].bitcast(FP8X4),
-                        rhs_scale=v_planes[a][:, cols],
+                        rhs_scale=v_s[a][:, cols],
                         start=(a == 0),
                         stop=(a == PASSES - 1),
                     )
-            u = u_tiles[unit % 4][:].rearrange("p (n t) -> p n t", t=PACK)
+            total = sum_tiles[unit % SUM_TILES][:].rearrange("p (n i) -> p n i", i=PACK)
             nc.vector.scalar_tensor_tensor(
-                out=u,
-                in0=wave[unit % NWAVE][:].rearrange("p (n t) -> p n t", t=PACK),
+                out=total,
+                in0=sine_tiles[unit % SINE_TILES][:].rearrange("p (n i) -> p n i", i=PACK),
                 scalar=2.0,
-                in1=bank[:].rearrange("p t n -> p n t"),
+                in1=bank[:].rearrange("p i n -> p n i"),
                 op0=ALU.mult,
                 op1=ALU.add,
             )
-            nc.scalar.activation(out=u, in_=u, func=ACT.Tanh, bias=minus_one[:])
-            h_bf = h_tiles[unit % 3]
-            nc.vector.tensor_tensor(
-                out=h_bf[:].rearrange("p (n t) -> p n t", t=PACK),
-                in0=u,
-                in1=gain_t[:, b, :].unsqueeze(1).to_broadcast([P, JC, PACK]),
-                op=ALU.mult,
-            )
+            nc.scalar.activation(out=total, in_=total, func=ACT.Tanh, bias=minus_one[:])
+            h_bf = h_tiles[unit % H_TILES]
+            if unit == UNITS - 1:
+                for i in range(PACK):
+                    nc.scalar.activation(
+                        out=h_by_deal[:, i, :], in_=total[:, :, i], func=ACT.Copy, scale=gain_t[:, b, i : i + 1]
+                    )
+                nc.scalar.copy(
+                    out=h_bf[:].rearrange("p (n i) -> p n i", i=PACK), in_=h_by_deal[:].rearrange("p i n -> p n i")
+                )
+            else:
+                nc.vector.tensor_tensor(
+                    out=h_bf[:].rearrange("p (n i) -> p n i", i=PACK),
+                    in0=total,
+                    in1=gain_t[:, b, :].unsqueeze(1).to_broadcast([P, JC, PACK]),
+                    op=ALU.mult,
+                )
             nc.vector.quantize_mx(
                 out=h_w[b][:, cols].bitcast(FP8X4),
                 scales=h_s[b][:, cols],
@@ -217,61 +236,57 @@ def tile_list_pace_note_grading_kernel(
 
         def direct(m):
             rows = slice(P * m, P * (m + 1))
-            bank = score_banks[m % 2]
+            bank = score_banks[m % SCORE_BANKS]
             for a in range(PASSES):
                 nc.tensor.matmul_mx(
                     out=bank[:],
                     lhsT=v2_w[a][:, rows].bitcast(FP8X4),
                     lhsT_scale=v2_s[4 * a : P, rows],
                     rhs=v_w[a][:].bitcast(FP8X4),
-                    rhs_scale=v_planes[a][:],
+                    rhs_scale=v_s[a][:],
                     start=(a == 0),
                     stop=(a == PASSES - 1),
                 )
-            nc.vector.tensor_tensor(out=dw[m][:], in0=bank[:], in1=wgo_t[:], op=ALU.mult)
+            nc.vector.tensor_tensor(out=d_wgo[m][:], in0=bank[:], in1=wgo_t[:], op=ALU.mult)
 
-        def grade(m, c0, c1):
+        def grade(m, group):
             rows = slice(P * m, P * (m + 1))
-            cols = slice(JC * c0, JC * c1)
-            width = JC * (c1 - c0)
-            bank = score_banks[m % 2]
-            for b in range(2):
+            cols = slice(GROUP * group, GROUP * (group + 1))
+            bank = score_banks[m % SCORE_BANKS]
+            for b in range(HALVES):
                 nc.tensor.matmul_mx(
-                    out=bank[:, 0:width],
+                    out=bank[:, 0:GROUP],
                     lhsT=v2_w[b][:, rows].bitcast(FP8X4),
                     lhsT_scale=v2_s[4 * b : P, rows],
                     rhs=h_w[b][:, cols].bitcast(FP8X4),
                     rhs_scale=h_s[b][:, cols],
                     start=(b == 0),
-                    stop=(b == 1),
+                    stop=(b == HALVES - 1),
                 )
-            tile_of = {(0, 0): 1, (0, 1): 3, (2, 0): 0, (2, 1): 2}[c0, m // 2]
-            score = u_tiles[tile_of][:, width * (m % 2) : width * (m % 2 + 1)]
-            nc.scalar.activation(out=score, in_=bank[:, 0:width], func=ACT.Tanh, bias=bias_t[:, m : m + 1])
+            score = sum_tiles[2 * (m // 2) + 1 - group][:, GROUP * (m % 2) : GROUP * (m % 2 + 1)]
+            nc.scalar.activation(out=score, in_=bank[:, 0:GROUP], func=ACT.Tanh, bias=bias_t[:, m : m + 1])
             nc.vector.tensor_tensor(
-                page[m][:].indirect(idx3[:, JC * c0 // 16 : JC * c1 // 16]),
+                page[m][:].indirect(idx3[:, cols.start // LIST_ROWS : cols.stop // LIST_ROWS]),
                 score,
-                dw[m][:, cols],
+                d_wgo[m][:, cols],
                 ALU.mult,
             )
 
         nc.vector.tensor_copy(v2_s[:], tab2_s[:].indirect(idx2[:]))
-        for a in range(PASSES):
-            nc.vector.tensor_copy(v2_w[a][:], tab2_w[a][:].bitcast(U32).indirect(idx2[:]))
+        for b in range(HALVES):
+            nc.vector.tensor_copy(v2_w[b][:], tab2_w[b][:].bitcast(U32).indirect(idx2[:]))
         for m in range(MT):
             direct(m)
-        for b in range(2):
-            for a in range(PASSES):
-                cast_w1(b, a)
-                quantize_w1(b, a)
-        units = [(b, c) for b in range(2) for c in range(CHUNKS)]
-        bend(*units[0])
-        for i, unit in enumerate(units):
-            if i + 1 < len(units):
-                bend(*units[i + 1])
-            features(*unit)
-        for c0, c1 in GROUPS:
+        for b, a in blocks:
+            quantize_w1(b, a)
+        bend(0)
+        for unit in range(UNITS):
+            if unit + 1 < UNITS:
+                bend(unit + 1)
+            features(unit)
+        groups = S // GROUP
+        for group in range(groups):
             for m in range(MT):
-                grade(m, c0, c1)
-                if c1 == CHUNKS:
+                grade(m, group)
+                if group == groups - 1:
                     nc.sync.dma_start(out=out[P * m : P * (m + 1), :], in_=page[m][:])

import math
from contextlib import ExitStack

import concourse.mybir as mybir

K, T, S, H, S2, T3, T2 = 1024, 2048, 512, 1024, 512, 2048, 1024
FLOPS = 2 * (2 * K * H * S + 2 * H * S2 * S)

F32 = mybir.dt.float32
BF16 = mybir.dt.bfloat16
I32 = mybir.dt.int32
U32 = mybir.dt.uint32
U16 = mybir.dt.uint16
U8 = mybir.dt.uint8
FP8X4 = mybir.dt.float8_e4m3fn_x4
FP4X4 = mybir.dt.float4_e2m1fn_x4
ACT = mybir.ActivationFunctionType
ALU = mybir.AluOpType

P = 128
PACK = 4
KP = P * PACK
PASSES = K // KP
HALVES = H // KP
QUADS = 4
LIST_ROWS = 16
JC = 128
CHUNKS = S // JC
UNITS = HALVES * CHUNKS
MT = S2 // P
GROUP = 2 * JC

VECTOR_CAST = {(0, 0): 128, (0, 1): 128, (1, 0): 0, (1, 1): 96}

SINE_TILES = 2
SUM_TILES = 4
H_TILES = 3
BEND_BANKS, LINE_BANKS, SCORE_BANKS = 3, 3, 2


def tile_list_pace_note_grading_kernel(
    tc, tab_words, tab_scales, offs, tab2_words, tab2_scales, offs2, offs3,
    w4_words, w4_scales, w1, gain, bias, wgo, page1, out,
):
    nc = tc.nc
    with ExitStack() as ctx:
        keep = ctx.enter_context(tc.tile_pool(name="keep", bufs=1))
        psum = ctx.enter_context(tc.psum_pool(name="psum", bufs=1))

        def kept(shape, dtype, name):
            return keep.tile(shape, dtype, name=name, align_bytes=64)

        blocks = [(b, a) for b in range(HALVES) for a in range(PASSES)]
        idx = kept([P, S // LIST_ROWS], U16, "idx")
        idx2 = kept([P, S2 // LIST_ROWS], U16, "idx2")
        idx3 = kept([P, S // LIST_ROWS], U16, "idx3")
        tab_w = [kept([P, T], I32, "tab_w%d" % a) for a in range(PASSES)]
        tab2_w = [kept([P, T3], I32, "tab2_w%d" % b) for b in range(HALVES)]
        tab_s = kept([P, PASSES * T], U8, "tab_s")
        tab2_s = kept([P, T3], U8, "tab2_s")
        w4_w = kept([P, PASSES, 2 * H], U8, "w4_w")
        w4_s = kept([P, PASSES, H], U8, "w4_s")
        w4_dealt_w = kept([P, PASSES * 2 * H], U8, "w4_dealt_w")
        w4_dealt_s = kept([P, PASSES * H], U8, "w4_dealt_s")
        w1_raw = {ba: kept([P, PACK, KP], F32, "w1_raw%d%d" % ba) for ba in blocks}
        w1_bf = {ba: kept([P, PACK * KP], BF16, "w1_bf%d%d" % ba) for ba in blocks}
        w1_w = {ba: kept([P, KP], U32, "w1_w%d%d" % ba) for ba in blocks}
        w1_s = {ba: kept([P, KP], U8, "w1_s%d%d" % ba) for ba in blocks}
        v_w = [kept([P, S], U32, "v_w%d" % a) for a in range(PASSES)]
        v2_w = [kept([P, S2], U32, "v2_w%d" % b) for b in range(HALVES)]
        v_s = [kept([P, S], U8, "v_s%d" % a) for a in range(PASSES)]
        v2_s = kept([P, S2], U8, "v2_s")
        h_w = [kept([P, S], U32, "h_w%d" % b) for b in range(HALVES)]
        h_s = [kept([P, S], U8, "h_s%d" % b) for b in range(HALVES)]
        gain_t = kept([P, HALVES, PACK], F32, "gain_t")
        bias_t = kept([P, MT], F32, "bias_t")
        wgo_t = kept([P, S], F32, "wgo_t")
        d_wgo = [kept([P, S], F32, "d_wgo%d" % m) for m in range(MT)]
        page = [kept([P, T2], F32, "page%d" % m) for m in range(MT)]
        plus_one = kept([P, 1], F32, "plus_one")
        minus_one = kept([P, 1], F32, "minus_one")
        shift = kept([P, 1], F32, "shift")
        sine_tiles = [kept([P, PACK * JC], F32, "sine%d" % n) for n in range(SINE_TILES)]
        sum_tiles = [kept([P, PACK * JC], F32, "sum%d" % n) for n in range(SUM_TILES)]
        h_tiles = [kept([P, PACK * JC], BF16, "h_bf%d" % n) for n in range(H_TILES)]
        h_by_deal = kept([P, PACK, JC], BF16, "h_by_deal")
        bend_banks = [psum.tile([P, PACK, JC], F32, name="bend_bank%d" % n) for n in range(BEND_BANKS)]
        line_banks = [psum.tile([P, PACK, JC], F32, name="line_bank%d" % n) for n in range(LINE_BANKS)]
        score_banks = [psum.tile([P, S], F32, name="score_bank%d" % n) for n in range(SCORE_BANKS)]

        def words(dram, a):
            return dram[a].rearrange("p n i -> p (n i)").bitcast(I32)

        def load_w1(b, a):
            rows = w1[KP * a : KP * (a + 1), KP * b : KP * (b + 1)]
            nc.sync.dma_start(out=w1_raw[b, a][:], in_=rows.rearrange("(p j) c -> p j c", j=PACK))

        nc.vector.memset(tab_s[:].bitcast(I32), 0)
        nc.gpsimd.memset(w4_s[:].rearrange("p a n -> p (a n)").bitcast(I32), 0)
        nc.gpsimd.memset(tab2_s[:].bitcast(I32), 0)
        nc.vector.memset(plus_one[:], 1.0)
        nc.vector.memset(minus_one[:], -1.0)
        nc.vector.tensor_scalar(out=shift[:], in0=plus_one[:], scalar1=-math.pi / 8, scalar2=None, op0=ALU.mult)
        warm = kept([P, 1], F32, "warm")
        nc.scalar.activation(out=warm[:], in_=plus_one[:], func=ACT.Silu)

        nc.sync.dma_start(idx[:], offs)
        nc.sync.dma_start(out=w4_w[:].bitcast(I32), in_=w4_words.rearrange("a p n -> p a n").bitcast(I32))
        for q in range(QUADS):
            nc.sync.dma_start(
                out=tab_s[32 * q : 32 * q + 4, :].bitcast(I32).rearrange("r (a n) -> r a n", a=PASSES),
                in_=tab_scales[:, 4 * q : 4 * q + 4, :].rearrange("a r n -> r a n").bitcast(I32),
            )
        for a in range(PASSES):
            nc.sync.dma_start(out=tab_w[a][:], in_=words(tab_words, a))
        for q in range(QUADS):
            nc.sync.dma_start(
                out=w4_s[32 * q : 32 * q + 4].bitcast(I32),
                in_=w4_scales[:, 4 * q : 4 * q + 4, :].rearrange("a r n -> r a n").bitcast(I32),
            )
        load_w1(0, 0)
        load_w1(0, 1)
        with nc.allow_non_contiguous_dma(reason="the four channels of a partition's word, for each half"):
            nc.sync.dma_start(out=gain_t[:], in_=gain.rearrange("(b p i) -> p b i", b=HALVES, i=PACK))
        load_w1(1, 0)
        nc.sync.dma_start(idx2[:], offs2)
        for q in range(QUADS):
            nc.sync.dma_start(
                out=tab2_s[32 * q : 32 * q + 8, :].bitcast(I32),
                in_=tab2_scales[:, 4 * q : 4 * q + 4, :].bitcast(I32),
            )
        nc.sync.dma_start(out=tab2_w[0][:], in_=words(tab2_words, 0))
        load_w1(1, 1)
        nc.sync.dma_start(out=tab2_w[1][:], in_=words(tab2_words, 1))
        nc.sync.dma_start(out=wgo_t[:], in_=wgo)
        nc.sync.dma_start(idx3[:], offs3)
        with nc.allow_non_contiguous_dma(reason="one value a partition for each tile of templates"):
            nc.sync.dma_start(out=bias_t[:], in_=bias.rearrange("(m p) -> p m", p=P))
        for m in range(MT):
            nc.sync.dma_start(out=page[m][:], in_=page1[P * m : P * (m + 1), :])

        nc.vector.tensor_copy(
            out=w4_dealt_w[:].bitcast(U16).rearrange("p (g i c) -> p g i c", i=PACK, c=P),
            in_=w4_w[:].rearrange("p a n -> p (a n)").bitcast(U16).rearrange("p (g c i) -> p g i c", i=PACK, c=P),
        )
        for a in range(PASSES):
            nc.vector.tensor_copy(v_s[a][:], tab_s[:, T * a : T * (a + 1)].indirect(idx[:]))
        nc.vector.tensor_copy(v_w[0][:], tab_w[0][:].bitcast(U32).indirect(idx[:]))
        nc.vector.tensor_copy(
            out=w4_dealt_s[:].rearrange("p (g i c) -> p g i c", i=PACK, c=P),
            in_=w4_s[:].rearrange("p a n -> p (a n)").rearrange("p (g c i) -> p g i c", i=PACK, c=P),
        )
        nc.vector.tensor_copy(v_w[1][:], tab_w[1][:].bitcast(U32).indirect(idx[:]))

        def quantize_w1(b, a):
            src = w1_raw[b, a][:].rearrange("p j (c i) -> p c j i", i=PACK)
            dst = w1_bf[b, a][:].rearrange("p (i c j) -> p c j i", i=PACK, j=PACK)
            cut = VECTOR_CAST[b, a]
            if cut > 0:
                nc.vector.tensor_copy(out=dst[:, 0:cut], in_=src[:, 0:cut])
            if cut < P:
                nc.scalar.copy(out=dst[:, cut:P], in_=src[:, cut:P])
            nc.vector.quantize_mx(out=w1_w[b, a][:].bitcast(FP8X4), scales=w1_s[b, a][:], in_=w1_bf[b, a][:])

        def bend(unit):
            b, chunk = divmod(unit, CHUNKS)
            cols = slice(JC * chunk, JC * (chunk + 1))
            bank = bend_banks[unit % BEND_BANKS]
            for i in range(PACK):
                for a in range(PASSES):
                    col = H * a + KP * b + P * i
                    nc.tensor.matmul_mx(
                        out=bank[:, i, :],
                        lhsT=w4_dealt_w[:, 2 * col : 2 * (col + P)].bitcast(FP4X4),
                        lhsT_scale=w4_dealt_s[:, col : col + P],
                        rhs=v_w[a][:, cols].bitcast(FP8X4),
                        rhs_scale=v_s[a][:, cols],
                        start=(a == 0),
                        stop=(a == PASSES - 1),
                    )
            sine = sine_tiles[unit % SINE_TILES]
            nc.scalar.activation(
                out=sine[:].rearrange("p (n i) -> p n i", i=PACK),
                in_=bank[:].rearrange("p i n -> p n i"),
                func=ACT.Sin, scale=0.25, bias=shift[:],
            )
            nc.scalar.activation(out=sine[:], in_=sine[:], func=ACT.Square)
            nc.scalar.activation(out=sine[:], in_=sine[:], func=ACT.Square, scale=-2.0, bias=plus_one[:])

        def features(unit):
            b, chunk = divmod(unit, CHUNKS)
            cols = slice(JC * chunk, JC * (chunk + 1))
            bank = line_banks[unit % LINE_BANKS]
            for i in range(PACK):
                for a in range(PASSES):
                    nc.tensor.matmul_mx(
                        out=bank[:, i, :],
                        lhsT=w1_w[b, a][:, P * i : P * (i + 1)].bitcast(FP8X4),
                        lhsT_scale=w1_s[b, a][:, P * i : P * (i + 1)],
                        rhs=v_w[a][:, cols].bitcast(FP8X4),
                        rhs_scale=v_s[a][:, cols],
                        start=(a == 0),
                        stop=(a == PASSES - 1),
                    )
            total = sum_tiles[unit % SUM_TILES][:].rearrange("p (n i) -> p n i", i=PACK)
            nc.vector.scalar_tensor_tensor(
                out=total,
                in0=sine_tiles[unit % SINE_TILES][:].rearrange("p (n i) -> p n i", i=PACK),
                scalar=2.0,
                in1=bank[:].rearrange("p i n -> p n i"),
                op0=ALU.mult,
                op1=ALU.add,
            )
            nc.scalar.activation(out=total, in_=total, func=ACT.Tanh, bias=minus_one[:])
            h_bf = h_tiles[unit % H_TILES]
            if unit == UNITS - 1:
                for i in range(PACK):
                    nc.scalar.activation(
                        out=h_by_deal[:, i, :], in_=total[:, :, i], func=ACT.Copy, scale=gain_t[:, b, i : i + 1]
                    )
                nc.scalar.copy(
                    out=h_bf[:].rearrange("p (n i) -> p n i", i=PACK), in_=h_by_deal[:].rearrange("p i n -> p n i")
                )
            else:
                nc.vector.tensor_tensor(
                    out=h_bf[:].rearrange("p (n i) -> p n i", i=PACK),
                    in0=total,
                    in1=gain_t[:, b, :].unsqueeze(1).to_broadcast([P, JC, PACK]),
                    op=ALU.mult,
                )
            nc.vector.quantize_mx(
                out=h_w[b][:, cols].bitcast(FP8X4),
                scales=h_s[b][:, cols],
                in_=h_bf[:],
            )

        def direct(m):
            rows = slice(P * m, P * (m + 1))
            bank = score_banks[m % SCORE_BANKS]
            for a in range(PASSES):
                nc.tensor.matmul_mx(
                    out=bank[:],
                    lhsT=v2_w[a][:, rows].bitcast(FP8X4),
                    lhsT_scale=v2_s[4 * a : P, rows],
                    rhs=v_w[a][:].bitcast(FP8X4),
                    rhs_scale=v_s[a][:],
                    start=(a == 0),
                    stop=(a == PASSES - 1),
                )
            nc.vector.tensor_tensor(out=d_wgo[m][:], in0=bank[:], in1=wgo_t[:], op=ALU.mult)

        def grade(m, group):
            rows = slice(P * m, P * (m + 1))
            cols = slice(GROUP * group, GROUP * (group + 1))
            bank = score_banks[m % SCORE_BANKS]
            for b in range(HALVES):
                nc.tensor.matmul_mx(
                    out=bank[:, 0:GROUP],
                    lhsT=v2_w[b][:, rows].bitcast(FP8X4),
                    lhsT_scale=v2_s[4 * b : P, rows],
                    rhs=h_w[b][:, cols].bitcast(FP8X4),
                    rhs_scale=h_s[b][:, cols],
                    start=(b == 0),
                    stop=(b == HALVES - 1),
                )
            score = sum_tiles[2 * (m // 2) + 1 - group][:, GROUP * (m % 2) : GROUP * (m % 2 + 1)]
            nc.scalar.activation(out=score, in_=bank[:, 0:GROUP], func=ACT.Tanh, bias=bias_t[:, m : m + 1])
            nc.vector.tensor_tensor(
                page[m][:].indirect(idx3[:, cols.start // LIST_ROWS : cols.stop // LIST_ROWS]),
                score,
                d_wgo[m][:, cols],
                ALU.mult,
            )

        nc.vector.tensor_copy(v2_s[:], tab2_s[:].indirect(idx2[:]))
        for b in range(HALVES):
            nc.vector.tensor_copy(v2_w[b][:], tab2_w[b][:].bitcast(U32).indirect(idx2[:]))
        for m in range(MT):
            direct(m)
        for b, a in blocks:
            quantize_w1(b, a)
        bend(0)
        for unit in range(UNITS):
            if unit + 1 < UNITS:
                bend(unit + 1)
            features(unit)
        groups = S // GROUP
        for group in range(groups):
            for m in range(MT):
                grade(m, group)
                if group == groups - 1:
                    nc.sync.dma_start(out=out[P * m : P * (m + 1), :], in_=page[m][:])
